import numpy as np
import ml_dtypes

BF16 = ml_dtypes.bfloat16


def bf(x):
    return np.asarray(x, np.float32).astype(BF16)


def f32(x):
    return np.asarray(x, np.float32)


def f64(x):
    return np.asarray(x).astype(np.float64)


def striped(idx):
    return np.tile(idx.reshape(-1, 16).T, (8, 1))


S, K, M, N, D, V = 2048, 256, 128, 1024, 4, 256


def setup_inputs():
    return {"table": bf(np.random.standard_normal((K, S))), "w": bf(np.random.standard_normal((D, K, M)) / np.sqrt(D * K)), "b": f32(0.5 * np.random.standard_normal((M, 1))), "offs": striped(np.random.permutation(np.tile(np.arange(S), 2))[:N])}


def reference(table, w, b, offs):
    idx = offs[:16].T.reshape(-1)
    x = f64(table)[:, idx]
    y = sum(f64(w)[t].T @ x[:, t * V : (t + 1) * V] for t in range(D))
    return y + f64(b)

@@ -1,0 +1,54 @@
+import concourse.mybir as mybir
+
+BF16, F32, U16 = mybir.dt.bfloat16, mybir.dt.float32, mybir.dt.uint16
+
+P = 128
+S = 2048
+K = 256
+M = 128
+RELATIONS = 4
+V = 256
+K_BLOCKS = K // P
+PIECE_COLUMNS = V // 16
+
+FLOPS = 2 * RELATIONS * K * M * V
+
+
+def tile_gather_matmul_kernel(tc, table, w, b, offs, out):
+    nc = tc.nc
+    with (
+        tc.tile_pool(name="held", bufs=1) as held,
+        tc.psum_pool(name="psum", bufs=1) as psum,
+    ):
+        offsets = held.tile([P, RELATIONS * PIECE_COLUMNS], U16, name="offsets")
+        nc.sync.dma_start(offsets[:], offs)
+
+        blocks = []
+        for a in range(K_BLOCKS):
+            block = held.tile([P, S], BF16, name="block%d" % a)
+            nc.sync.dma_start(block[:], table[a * P : (a + 1) * P, :])
+            blocks.append(block)
+
+        weights = held.tile([P, RELATIONS * K_BLOCKS, M], BF16, name="weights")
+        nc.scalar.dma_start(weights[:], w.rearrange("t (a p) m -> p (t a) m", p=P))
+
+        bias = held.tile([P, 1], F32, name="bias")
+        nc.scalar.dma_start(bias[:], b)
+
+        y = psum.tile([M, V], F32, name="y")
+        last = K_BLOCKS * RELATIONS - 1
+        for a in range(K_BLOCKS):
+            for t in range(RELATIONS):
+                piece = offsets[:, t * PIECE_COLUMNS : (t + 1) * PIECE_COLUMNS]
+                step = a * RELATIONS + t
+                nc.tensor.matmul(
+                    y[:],
+                    weights[:, t * K_BLOCKS + a, :],
+                    blocks[a][:].indirect(piece),
+                    start=(step == 0),
+                    stop=(step == last),
+                )
+
+        result = held.tile([M, V], F32, name="result")
+        nc.vector.tensor_scalar_add(result[:], y[:], bias[:, 0:1])
+        nc.sync.dma_start(out, result[:])

@@ -11,6 +11,9 @@ V = 256
 K_BLOCKS = K // P
 PIECE_COLUMNS = V // 16
 
+WARM_COLUMNS = 512
+WARM_MATMULS = 8
+
 FLOPS = 2 * RELATIONS * K * M * V
 
 
@@ -34,6 +37,12 @@ def tile_gather_matmul_kernel(tc, table, w, b, offs, out):
 
         bias = held.tile([P, 1], F32, name="bias")
         nc.scalar.dma_start(bias[:], b)
+
+        zeros = held.tile([P, WARM_COLUMNS], BF16, name="zeros")
+        nc.vector.memset(zeros[:], 0.0)
+        unread = psum.tile([P, WARM_COLUMNS], F32, name="unread")
+        for i in range(WARM_MATMULS):
+            nc.tensor.matmul(unread[:], zeros[:, 0:P], zeros[:], start=True, stop=True)
 
         y = psum.tile([M, V], F32, name="y")
         last = K_BLOCKS * RELATIONS - 1

@@ -10,9 +10,7 @@ RELATIONS = 4
 V = 256
 K_BLOCKS = K // P
 PIECE_COLUMNS = V // 16
-
-WARM_COLUMNS = 512
-WARM_MATMULS = 8
+HALF = RELATIONS // 2
 
 FLOPS = 2 * RELATIONS * K * M * V
 
@@ -26,23 +24,18 @@ def tile_gather_matmul_kernel(tc, table, w, b, offs, out):
         offsets = held.tile([P, RELATIONS * PIECE_COLUMNS], U16, name="offsets")
         nc.sync.dma_start(offsets[:], offs)
 
-        blocks = []
-        for a in range(K_BLOCKS):
-            block = held.tile([P, S], BF16, name="block%d" % a)
-            nc.sync.dma_start(block[:], table[a * P : (a + 1) * P, :])
-            blocks.append(block)
+        table_by_block = table.rearrange("(p a) s -> a p s", a=K_BLOCKS)
+        w_by_partition = w.rearrange("t (p a) m -> p t (a m)", a=K_BLOCKS)
 
-        weights = held.tile([P, RELATIONS * K_BLOCKS, M], BF16, name="weights")
-        nc.scalar.dma_start(weights[:], w.rearrange("t (a p) m -> p (t a) m", p=P))
-
+        blocks = [held.tile([P, S], BF16, name="block%d" % a) for a in range(K_BLOCKS)]
+        weights = [held.tile([P, HALF, K_BLOCKS * M], BF16, name="weights%d" % h) for h in range(2)]
         bias = held.tile([P, 1], F32, name="bias")
-        nc.scalar.dma_start(bias[:], b)
 
-        zeros = held.tile([P, WARM_COLUMNS], BF16, name="zeros")
-        nc.vector.memset(zeros[:], 0.0)
-        unread = psum.tile([P, WARM_COLUMNS], F32, name="unread")
-        for i in range(WARM_MATMULS):
-            nc.tensor.matmul(unread[:], zeros[:, 0:P], zeros[:], start=True, stop=True)
+        nc.scalar.dma_start(blocks[0][:], table_by_block[0])
+        nc.sync.dma_start(weights[0][:], w_by_partition[:, 0:HALF, :])
+        nc.scalar.dma_start(weights[1][:], w_by_partition[:, HALF:RELATIONS, :])
+        nc.scalar.dma_start(blocks[1][:], table_by_block[1])
+        nc.scalar.dma_start(bias[:], b)
 
         y = psum.tile([M, V], F32, name="y")
         last = K_BLOCKS * RELATIONS - 1
@@ -52,7 +45,7 @@ def tile_gather_matmul_kernel(tc, table, w, b, offs, out):
                 step = a * RELATIONS + t
                 nc.tensor.matmul(
                     y[:],
-                    weights[:, t * K_BLOCKS + a, :],
+                    weights[t // HALF][:, t % HALF, a * M : (a + 1) * M],
                     blocks[a][:].indirect(piece),
                     start=(step == 0),
                     stop=(step == last),

@@ -10,7 +10,6 @@ RELATIONS = 4
 V = 256
 K_BLOCKS = K // P
 PIECE_COLUMNS = V // 16
-HALF = RELATIONS // 2
 
 FLOPS = 2 * RELATIONS * K * M * V
 
@@ -25,27 +24,35 @@ def tile_gather_matmul_kernel(tc, table, w, b, offs, out):
         nc.sync.dma_start(offsets[:], offs)
 
         table_by_block = table.rearrange("(p a) s -> a p s", a=K_BLOCKS)
-        w_by_partition = w.rearrange("t (p a) m -> p t (a m)", a=K_BLOCKS)
+        w_by_block = w.rearrange("t (p a) m -> a p t m", a=K_BLOCKS)
 
         blocks = [held.tile([P, S], BF16, name="block%d" % a) for a in range(K_BLOCKS)]
-        weights = [held.tile([P, HALF, K_BLOCKS * M], BF16, name="weights%d" % h) for h in range(2)]
+        first_weights = held.tile([P, K_BLOCKS * M], BF16, name="first_weights")
+        later_weights = [
+            held.tile([P, RELATIONS - 1, M], BF16, name="later_weights%d" % a) for a in range(K_BLOCKS)
+        ]
         bias = held.tile([P, 1], F32, name="bias")
 
         nc.scalar.dma_start(blocks[0][:], table_by_block[0])
-        nc.sync.dma_start(weights[0][:], w_by_partition[:, 0:HALF, :])
-        nc.scalar.dma_start(weights[1][:], w_by_partition[:, HALF:RELATIONS, :])
+        nc.sync.dma_start(first_weights[:], w.rearrange("t (p a) m -> p t (a m)", a=K_BLOCKS)[:, 0, :])
+        nc.sync.dma_start(bias[:], b)
+        nc.scalar.dma_start(later_weights[0][:], w_by_block[0][:, 1:RELATIONS, :])
         nc.scalar.dma_start(blocks[1][:], table_by_block[1])
-        nc.scalar.dma_start(bias[:], b)
+        nc.scalar.dma_start(later_weights[1][:], w_by_block[1][:, 1:RELATIONS, :])
 
         y = psum.tile([M, V], F32, name="y")
         last = K_BLOCKS * RELATIONS - 1
         for a in range(K_BLOCKS):
             for t in range(RELATIONS):
                 piece = offsets[:, t * PIECE_COLUMNS : (t + 1) * PIECE_COLUMNS]
+                if t == 0:
+                    weights = first_weights[:, a * M : (a + 1) * M]
+                else:
+                    weights = later_weights[a][:, t - 1, :]
                 step = a * RELATIONS + t
                 nc.tensor.matmul(
                     y[:],
-                    weights[t // HALF][:, t % HALF, a * M : (a + 1) * M],
+                    weights,
                     blocks[a][:].indirect(piece),
                     start=(step == 0),
                     stop=(step == last),

@@ -10,6 +10,8 @@ RELATIONS = 4
 V = 256
 K_BLOCKS = K // P
 PIECE_COLUMNS = V // 16
+BANK = 512
+WARM_UPS = 6
 
 FLOPS = 2 * RELATIONS * K * M * V
 
@@ -39,6 +41,12 @@ def tile_gather_matmul_kernel(tc, table, w, b, offs, out):
         nc.scalar.dma_start(later_weights[0][:], w_by_block[0][:, 1:RELATIONS, :])
         nc.scalar.dma_start(blocks[1][:], table_by_block[1])
         nc.scalar.dma_start(later_weights[1][:], w_by_block[1][:, 1:RELATIONS, :])
+
+        zeros = held.tile([P, BANK], BF16, name="zeros")
+        nc.vector.memset(zeros[:], 0.0)
+        unread = psum.tile([M, BANK], F32, name="unread")
+        for i in range(WARM_UPS):
+            nc.tensor.matmul(unread[:], zeros[:, 0:M], zeros[:], start=True, stop=True)
 
         y = psum.tile([M, V], F32, name="y")
         last = K_BLOCKS * RELATIONS - 1

@@ -23,7 +23,6 @@ def tile_gather_matmul_kernel(tc, table, w, b, offs, out):
         tc.psum_pool(name="psum", bufs=1) as psum,
     ):
         offsets = held.tile([P, RELATIONS * PIECE_COLUMNS], U16, name="offsets")
-        nc.sync.dma_start(offsets[:], offs)
 
         table_by_block = table.rearrange("(p a) s -> a p s", a=K_BLOCKS)
         w_by_block = w.rearrange("t (p a) m -> a p t m", a=K_BLOCKS)
@@ -35,9 +34,10 @@ def tile_gather_matmul_kernel(tc, table, w, b, offs, out):
         ]
         bias = held.tile([P, 1], F32, name="bias")
 
-        nc.scalar.dma_start(blocks[0][:], table_by_block[0])
-        nc.sync.dma_start(first_weights[:], w.rearrange("t (p a) m -> p t (a m)", a=K_BLOCKS)[:, 0, :])
+        nc.sync.dma_start(blocks[0][:], table_by_block[0])
+        nc.sync.dma_start(offsets[:], offs)
         nc.sync.dma_start(bias[:], b)
+        nc.scalar.dma_start(first_weights[:], w.rearrange("t (p a) m -> p t (a m)", a=K_BLOCKS)[:, 0, :])
         nc.scalar.dma_start(later_weights[0][:], w_by_block[0][:, 1:RELATIONS, :])
         nc.scalar.dma_start(blocks[1][:], table_by_block[1])
         nc.scalar.dma_start(later_weights[1][:], w_by_block[1][:, 1:RELATIONS, :])

@@ -11,7 +11,7 @@ V = 256
 K_BLOCKS = K // P
 PIECE_COLUMNS = V // 16
 BANK = 512
-WARM_UPS = 6
+WARM_UPS = 4
 
 FLOPS = 2 * RELATIONS * K * M * V
 

@@ -36,11 +36,11 @@ def tile_gather_matmul_kernel(tc, table, w, b, offs, out):
 
         nc.sync.dma_start(blocks[0][:], table_by_block[0])
         nc.sync.dma_start(offsets[:], offs)
-        nc.sync.dma_start(bias[:], b)
         nc.scalar.dma_start(first_weights[:], w.rearrange("t (p a) m -> p t (a m)", a=K_BLOCKS)[:, 0, :])
         nc.scalar.dma_start(later_weights[0][:], w_by_block[0][:, 1:RELATIONS, :])
         nc.scalar.dma_start(blocks[1][:], table_by_block[1])
         nc.scalar.dma_start(later_weights[1][:], w_by_block[1][:, 1:RELATIONS, :])
+        nc.scalar.dma_start(bias[:], b)
 
         zeros = held.tile([P, BANK], BF16, name="zeros")
         nc.vector.memset(zeros[:], 0.0)

@@ -2,6 +2,8 @@ import concourse.mybir as mybir
 
 BF16, F32, U16 = mybir.dt.bfloat16, mybir.dt.float32, mybir.dt.uint16
 
+IDENTITY = mybir.ActivationFunctionType.Identity
+
 P = 128
 S = 2048
 K = 256
@@ -48,6 +50,10 @@ def tile_gather_matmul_kernel(tc, table, w, b, offs, out):
         for i in range(WARM_UPS):
             nc.tensor.matmul(unread[:], zeros[:, 0:M], zeros[:], start=True, stop=True)
 
+        scratch = held.tile([P, 1], F32, name="scratch")
+        nc.vector.memset(scratch[:], 0.0)
+        nc.scalar.activation(scratch[:], scratch[:], IDENTITY)
+
         y = psum.tile([M, V], F32, name="y")
         last = K_BLOCKS * RELATIONS - 1
         for a in range(K_BLOCKS):
@@ -67,5 +73,5 @@ def tile_gather_matmul_kernel(tc, table, w, b, offs, out):
                 )
 
         result = held.tile([M, V], F32, name="result")
-        nc.vector.tensor_scalar_add(result[:], y[:], bias[:, 0:1])
-        nc.sync.dma_start(out, result[:])
+        nc.scalar.activation(result[:], y[:], IDENTITY, bias=bias[:, 0:1])
+        nc.scalar.dma_start(out, result[:])

import concourse.mybir as mybir

BF16, F32, U16 = mybir.dt.bfloat16, mybir.dt.float32, mybir.dt.uint16

IDENTITY = mybir.ActivationFunctionType.Identity

P = 128
S = 2048
K = 256
M = 128
RELATIONS = 4
V = 256
K_BLOCKS = K // P
PIECE_COLUMNS = V // 16
BANK = 512
WARM_UPS = 4

FLOPS = 2 * RELATIONS * K * M * V


def tile_gather_matmul_kernel(tc, table, w, b, offs, out):
    nc = tc.nc
    with (
        tc.tile_pool(name="held", bufs=1) as held,
        tc.psum_pool(name="psum", bufs=1) as psum,
    ):
        offsets = held.tile([P, RELATIONS * PIECE_COLUMNS], U16, name="offsets")

        table_by_block = table.rearrange("(p a) s -> a p s", a=K_BLOCKS)
        w_by_block = w.rearrange("t (p a) m -> a p t m", a=K_BLOCKS)

        blocks = [held.tile([P, S], BF16, name="block%d" % a) for a in range(K_BLOCKS)]
        first_weights = held.tile([P, K_BLOCKS * M], BF16, name="first_weights")
        later_weights = [
            held.tile([P, RELATIONS - 1, M], BF16, name="later_weights%d" % a) for a in range(K_BLOCKS)
        ]
        bias = held.tile([P, 1], F32, name="bias")

        nc.sync.dma_start(blocks[0][:], table_by_block[0])
        nc.sync.dma_start(offsets[:], offs)
        nc.scalar.dma_start(first_weights[:], w.rearrange("t (p a) m -> p t (a m)", a=K_BLOCKS)[:, 0, :])
        nc.scalar.dma_start(later_weights[0][:], w_by_block[0][:, 1:RELATIONS, :])
        nc.scalar.dma_start(blocks[1][:], table_by_block[1])
        nc.scalar.dma_start(later_weights[1][:], w_by_block[1][:, 1:RELATIONS, :])
        nc.scalar.dma_start(bias[:], b)

        zeros = held.tile([P, BANK], BF16, name="zeros")
        nc.vector.memset(zeros[:], 0.0)
        unread = psum.tile([M, BANK], F32, name="unread")
        for i in range(WARM_UPS):
            nc.tensor.matmul(unread[:], zeros[:, 0:M], zeros[:], start=True, stop=True)

        scratch = held.tile([P, 1], F32, name="scratch")
        nc.vector.memset(scratch[:], 0.0)
        nc.scalar.activation(scratch[:], scratch[:], IDENTITY)

        y = psum.tile([M, V], F32, name="y")
        last = K_BLOCKS * RELATIONS - 1
        for a in range(K_BLOCKS):
            for t in range(RELATIONS):
                piece = offsets[:, t * PIECE_COLUMNS : (t + 1) * PIECE_COLUMNS]
                if t == 0:
                    weights = first_weights[:, a * M : (a + 1) * M]
                else:
                    weights = later_weights[a][:, t - 1, :]
                step = a * RELATIONS + t
                nc.tensor.matmul(
                    y[:],
                    weights,
                    blocks[a][:].indirect(piece),
                    start=(step == 0),
                    stop=(step == last),
                )

        result = held.tile([M, V], F32, name="result")
        nc.scalar.activation(result[:], y[:], IDENTITY, bias=bias[:, 0:1])
        nc.scalar.dma_start(out, result[:])
